import numpy as np
import ml_dtypes

BF16 = ml_dtypes.bfloat16


def bf(x):
    return np.asarray(x, np.float32).astype(BF16)


def f32(x):
    return np.asarray(x, np.float32)


def f64(x):
    return np.asarray(x).astype(np.float64)


def striped(idx):
    return np.tile(idx.reshape(-1, 16).T, (8, 1))


S, K, M, N, D, V = 4096, 512, 128, 2048, 4, 512


def setup_inputs():
    return {"table": bf(np.random.standard_normal((K, S))), "w": bf(np.random.standard_normal((K, M)) / np.sqrt(K)), "b": f32(0.5 * np.random.standard_normal((M, 1))), "offs": striped(np.random.permutation(S)[:N])}


def reference(table, w, b, offs):
    idx = offs[:16].T.reshape(-1)
    x = f64(table)[:, idx]
    y = f64(w).T @ x
    z = y + f64(b)
    return z.reshape(M, V, D).max(axis=2)

@@ -1,0 +1,63 @@
+import concourse.mybir as mybir
+
+BF16, F32, U16 = mybir.dt.bfloat16, mybir.dt.float32, mybir.dt.uint16
+
+P = 128
+K, S = 512, 4096
+M = 128
+N = 2048
+D = 4
+KB = K // P
+PIECE = 512
+PIECES = N // PIECE
+PIECE_OFFS = PIECE // 16
+PIECE_OUT = PIECE // D
+
+FLOPS = 2 * K * M * N
+BYTES = 2 * K * N + 2 * K * M + 4 * M + 2 * P * (N // 16) + 4 * M * (N // D)
+
+
+def tile_gather_matmul_kernel(tc, table, w, b, offs, out):
+    nc = tc.nc
+    with (
+        tc.tile_pool(name="held", bufs=1) as held,
+        tc.psum_pool(name="psum", bufs=1) as psum,
+    ):
+        offsets = held.tile([P, N // 16], U16, name="offsets")
+        nc.sync.dma_start(offsets[:], offs)
+
+        weights = held.tile([P, KB, M], BF16, name="weights")
+        nc.scalar.dma_start(weights[:], w.rearrange("(kb p) m -> p kb m", p=P))
+        bias = held.tile([P, 1], F32, name="bias")
+        nc.scalar.dma_start(bias[:], b)
+
+        blocks = [held.tile([P, S], BF16, name=f"block{kb}") for kb in range(KB)]
+        for kb in range(KB):
+            nc.sync.dma_start(blocks[kb][:], table[kb * P : (kb + 1) * P, :])
+
+        banks = [psum.tile([P, PIECE], F32, name=f"bank{piece}") for piece in range(PIECES)]
+        for kb in range(KB):
+            for piece in range(PIECES):
+                picked = blocks[kb][:].indirect(
+                    offsets[:, piece * PIECE_OFFS : (piece + 1) * PIECE_OFFS]
+                )
+                nc.tensor.matmul(
+                    banks[piece][:],
+                    weights[:, kb, :],
+                    picked,
+                    start=(kb == 0),
+                    stop=(kb == KB - 1),
+                )
+
+        pooled = held.tile([P, N // D], F32, name="pooled")
+        result = held.tile([P, N // D], F32, name="result")
+        for piece in range(PIECES):
+            cols = slice(piece * PIECE_OUT, (piece + 1) * PIECE_OUT)
+            nc.vector.tensor_reduce(
+                pooled[:, cols],
+                banks[piece][:].rearrange("p (v d) -> p v d", d=D),
+                axis=mybir.AxisListType.X,
+                op=mybir.AluOpType.max,
+            )
+            nc.vector.tensor_scalar_add(result[:, cols], pooled[:, cols], bias[:, 0:1])
+            nc.sync.dma_start(out[:, cols], result[:, cols])

@@ -12,6 +12,7 @@ PIECE = 512
 PIECES = N // PIECE
 PIECE_OFFS = PIECE // 16
 PIECE_OUT = PIECE // D
+WARM_UPS = 8
 
 FLOPS = 2 * K * M * N
 BYTES = 2 * K * N + 2 * K * M + 4 * M + 2 * P * (N // 16) + 4 * M * (N // D)
@@ -34,6 +35,12 @@ def tile_gather_matmul_kernel(tc, table, w, b, offs, out):
         blocks = [held.tile([P, S], BF16, name=f"block{kb}") for kb in range(KB)]
         for kb in range(KB):
             nc.sync.dma_start(blocks[kb][:], table[kb * P : (kb + 1) * P, :])
+
+        zeros = held.tile([P, PIECE], BF16, name="zeros")
+        nc.vector.memset(zeros[:], 0.0)
+        unused = psum.tile([P, PIECE], F32, name="unused")
+        for i in range(WARM_UPS):
+            nc.tensor.matmul(unused[:], zeros[:, 0:M], zeros[:], start=True, stop=True)
 
         banks = [psum.tile([P, PIECE], F32, name=f"bank{piece}") for piece in range(PIECES)]
         for kb in range(KB):

@@ -28,13 +28,14 @@ def tile_gather_matmul_kernel(tc, table, w, b, offs, out):
         nc.sync.dma_start(offsets[:], offs)
 
         weights = held.tile([P, KB, M], BF16, name="weights")
-        nc.scalar.dma_start(weights[:], w.rearrange("(kb p) m -> p kb m", p=P))
+        nc.scalar.dma_start(weights[:], w.rearrange("(p kb) m -> p kb m", kb=KB))
         bias = held.tile([P, 1], F32, name="bias")
         nc.scalar.dma_start(bias[:], b)
 
         blocks = [held.tile([P, S], BF16, name=f"block{kb}") for kb in range(KB)]
+        table_blocks = table.rearrange("(p kb) s -> kb p s", kb=KB)
         for kb in range(KB):
-            nc.sync.dma_start(blocks[kb][:], table[kb * P : (kb + 1) * P, :])
+            nc.sync.dma_start(blocks[kb][:], table_blocks[kb])
 
         zeros = held.tile([P, PIECE], BF16, name="zeros")
         nc.vector.memset(zeros[:], 0.0)

@@ -12,7 +12,6 @@ PIECE = 512
 PIECES = N // PIECE
 PIECE_OFFS = PIECE // 16
 PIECE_OUT = PIECE // D
-WARM_UPS = 8
 
 FLOPS = 2 * K * M * N
 BYTES = 2 * K * N + 2 * K * M + 4 * M + 2 * P * (N // 16) + 4 * M * (N // D)
@@ -36,12 +35,6 @@ def tile_gather_matmul_kernel(tc, table, w, b, offs, out):
         table_blocks = table.rearrange("(p kb) s -> kb p s", kb=KB)
         for kb in range(KB):
             nc.sync.dma_start(blocks[kb][:], table_blocks[kb])
-
-        zeros = held.tile([P, PIECE], BF16, name="zeros")
-        nc.vector.memset(zeros[:], 0.0)
-        unused = psum.tile([P, PIECE], F32, name="unused")
-        for i in range(WARM_UPS):
-            nc.tensor.matmul(unused[:], zeros[:, 0:M], zeros[:], start=True, stop=True)
 
         banks = [psum.tile([P, PIECE], F32, name=f"bank{piece}") for piece in range(PIECES)]
         for kb in range(KB):

@@ -36,6 +36,12 @@ def tile_gather_matmul_kernel(tc, table, w, b, offs, out):
         for kb in range(KB):
             nc.sync.dma_start(blocks[kb][:], table_blocks[kb])
 
+        spare = held.tile([P, 2], F32, name="spare")
+        nc.vector.memset(spare[:, 0:1], 0.0)
+        nc.scalar.activation(
+            spare[:, 1:2], spare[:, 0:1], mybir.ActivationFunctionType.Identity
+        )
+
         banks = [psum.tile([P, PIECE], F32, name=f"bank{piece}") for piece in range(PIECES)]
         for kb in range(KB):
             for piece in range(PIECES):
@@ -60,5 +66,13 @@ def tile_gather_matmul_kernel(tc, table, w, b, offs, out):
                 axis=mybir.AxisListType.X,
                 op=mybir.AluOpType.max,
             )
-            nc.vector.tensor_scalar_add(result[:, cols], pooled[:, cols], bias[:, 0:1])
+            if piece == PIECES - 1:
+                nc.vector.tensor_scalar_add(result[:, cols], pooled[:, cols], bias[:, 0:1])
+            else:
+                nc.scalar.activation(
+                    result[:, cols],
+                    pooled[:, cols],
+                    mybir.ActivationFunctionType.Identity,
+                    bias=bias[:, 0:1],
+                )
             nc.sync.dma_start(out[:, cols], result[:, cols])

@@ -26,8 +26,11 @@ def tile_gather_matmul_kernel(tc, table, w, b, offs, out):
         offsets = held.tile([P, N // 16], U16, name="offsets")
         nc.sync.dma_start(offsets[:], offs)
 
-        weights = held.tile([P, KB, M], BF16, name="weights")
-        nc.scalar.dma_start(weights[:], w.rearrange("(p kb) m -> p kb m", kb=KB))
+        w_rows = w.rearrange("(p kb) m -> p kb m", kb=KB)
+        first_weights = held.tile([P, M], BF16, name="first_weights")
+        nc.scalar.dma_start(first_weights[:], w_rows[:, 0, :])
+        later_weights = held.tile([P, KB - 1, M], BF16, name="later_weights")
+        weights = [first_weights[:]] + [later_weights[:, kb, :] for kb in range(KB - 1)]
         bias = held.tile([P, 1], F32, name="bias")
         nc.scalar.dma_start(bias[:], b)
 
@@ -35,6 +38,8 @@ def tile_gather_matmul_kernel(tc, table, w, b, offs, out):
         table_blocks = table.rearrange("(p kb) s -> kb p s", kb=KB)
         for kb in range(KB):
             nc.sync.dma_start(blocks[kb][:], table_blocks[kb])
+            if kb == 0:
+                nc.sync.dma_start(later_weights[:], w_rows[:, 1:, :])
 
         spare = held.tile([P, 2], F32, name="spare")
         nc.vector.memset(spare[:, 0:1], 0.0)
@@ -50,7 +55,7 @@ def tile_gather_matmul_kernel(tc, table, w, b, offs, out):
                 )
                 nc.tensor.matmul(
                     banks[piece][:],
-                    weights[:, kb, :],
+                    weights[kb],
                     picked,
                     start=(kb == 0),
                     stop=(kb == KB - 1),

import concourse.mybir as mybir

BF16, F32, U16 = mybir.dt.bfloat16, mybir.dt.float32, mybir.dt.uint16

P = 128
K, S = 512, 4096
M = 128
N = 2048
D = 4
KB = K // P
PIECE = 512
PIECES = N // PIECE
PIECE_OFFS = PIECE // 16
PIECE_OUT = PIECE // D

FLOPS = 2 * K * M * N
BYTES = 2 * K * N + 2 * K * M + 4 * M + 2 * P * (N // 16) + 4 * M * (N // D)


def tile_gather_matmul_kernel(tc, table, w, b, offs, out):
    nc = tc.nc
    with (
        tc.tile_pool(name="held", bufs=1) as held,
        tc.psum_pool(name="psum", bufs=1) as psum,
    ):
        offsets = held.tile([P, N // 16], U16, name="offsets")
        nc.sync.dma_start(offsets[:], offs)

        w_rows = w.rearrange("(p kb) m -> p kb m", kb=KB)
        first_weights = held.tile([P, M], BF16, name="first_weights")
        nc.scalar.dma_start(first_weights[:], w_rows[:, 0, :])
        later_weights = held.tile([P, KB - 1, M], BF16, name="later_weights")
        weights = [first_weights[:]] + [later_weights[:, kb, :] for kb in range(KB - 1)]
        bias = held.tile([P, 1], F32, name="bias")
        nc.scalar.dma_start(bias[:], b)

        blocks = [held.tile([P, S], BF16, name=f"block{kb}") for kb in range(KB)]
        table_blocks = table.rearrange("(p kb) s -> kb p s", kb=KB)
        for kb in range(KB):
            nc.sync.dma_start(blocks[kb][:], table_blocks[kb])
            if kb == 0:
                nc.sync.dma_start(later_weights[:], w_rows[:, 1:, :])

        spare = held.tile([P, 2], F32, name="spare")
        nc.vector.memset(spare[:, 0:1], 0.0)
        nc.scalar.activation(
            spare[:, 1:2], spare[:, 0:1], mybir.ActivationFunctionType.Identity
        )

        banks = [psum.tile([P, PIECE], F32, name=f"bank{piece}") for piece in range(PIECES)]
        for kb in range(KB):
            for piece in range(PIECES):
                picked = blocks[kb][:].indirect(
                    offsets[:, piece * PIECE_OFFS : (piece + 1) * PIECE_OFFS]
                )
                nc.tensor.matmul(
                    banks[piece][:],
                    weights[kb],
                    picked,
                    start=(kb == 0),
                    stop=(kb == KB - 1),
                )

        pooled = held.tile([P, N // D], F32, name="pooled")
        result = held.tile([P, N // D], F32, name="result")
        for piece in range(PIECES):
            cols = slice(piece * PIECE_OUT, (piece + 1) * PIECE_OUT)
            nc.vector.tensor_reduce(
                pooled[:, cols],
                banks[piece][:].rearrange("p (v d) -> p v d", d=D),
                axis=mybir.AxisListType.X,
                op=mybir.AluOpType.max,
            )
            if piece == PIECES - 1:
                nc.vector.tensor_scalar_add(result[:, cols], pooled[:, cols], bias[:, 0:1])
            else:
                nc.scalar.activation(
                    result[:, cols],
                    pooled[:, cols],
                    mybir.ActivationFunctionType.Identity,
                    bias=bias[:, 0:1],
                )
            nc.sync.dma_start(out[:, cols], result[:, cols])
